import numpy as np
import ml_dtypes


def mxq(x, axis, fmt="e4m3"):
    dtype, down = {"e4m3": (ml_dtypes.float8_e4m3fn, 7), "e5m2": (ml_dtypes.float8_e5m2, 14)}[fmt]
    v = np.moveaxis(np.asarray(x, np.float32).astype(ml_dtypes.bfloat16).astype(np.float64), axis, -1)
    blocks = v.reshape(v.shape[:-1] + (-1, 32))
    amax = np.abs(blocks).max(-1, keepdims=True)
    byte = np.maximum(np.where(amax > 0, np.frexp(amax)[1] - 1 + 127, 0) - down, 1)
    scale = np.exp2(byte - 127.0)
    codes = (blocks / scale).astype(np.float32).astype(dtype).astype(np.float64)
    return np.moveaxis((codes * scale).reshape(v.shape), -1, axis)


WIDE = False


def mx_kscale(k):
    if not WIDE:
        return np.ones(k)
    levels = np.array([10, -10, 5, -5, 0])
    if k % 512:
        return np.exp2(np.random.permutation(np.resize(levels, k // 32))).repeat(32)
    a = np.empty((k // 512, 16))
    for p in range(k // 512):
        a[p, :8] = np.random.permutation(np.resize(levels, 8))
        for g in range(8):
            far = levels[np.abs(levels - a[p, g]) >= 10]
            a[p, g + 8] = far[np.random.randint(len(far))]
    return np.exp2(a.ravel()).repeat(32)


def f64(x):
    return np.asarray(x).astype(np.float64)


def striped(idx):
    return np.tile(np.asarray(idx).reshape(-1, 16).T, (8, 1)).astype(np.uint16)


def unstriped(offs):
    return offs[:16].T.reshape(-1).astype(np.int64)


E2M1 = np.array([0.0, 0.5, 1.0, 1.5, 2.0, 3.0, 4.0, 6.0, -0.0, -0.5, -1.0, -1.5, -2.0, -3.0, -4.0, -6.0])


def pack_weight(w, fmt):
    k, n = w.shape
    w = f64(np.asarray(w, np.float32).astype(ml_dtypes.bfloat16)).reshape(k // 32, 32, n)
    amax = np.abs(w).max(1)
    if fmt == "e4m3":
        byte = np.frexp(amax)[1] - 1 + 127 - 7
    else:
        mant, ex = np.frexp(amax / 6.0)
        byte = np.where(mant > 0.5, ex, ex - 1) + 127
    byte = np.clip(np.where(amax > 0, byte, 1), 1, 254)
    scaled = (w * np.exp2(127.0 - byte)[:, None, :]).reshape(k, n).astype(np.float32)
    by_word = np.ascontiguousarray(scaled.reshape(k // 512, 128, 4, n).transpose(0, 1, 3, 2))
    if fmt == "e4m3":
        words = by_word.astype(ml_dtypes.float8_e4m3fn).view(np.uint8)
    else:
        c = by_word.astype(ml_dtypes.float4_e2m1fn).view(np.uint8) & 0xF
        words = (c[..., 0::2] | (c[..., 1::2] << 4)).reshape(k // 512, 128, 2 * n)
    return np.ascontiguousarray(words), np.ascontiguousarray(byte.astype(np.uint8).reshape(k // 512, 16, n))


def unpack_weight(words, scales, fmt):
    g, _, n = scales.shape
    words = np.ascontiguousarray(words).reshape(g, 128, n, -1)
    if fmt == "e4m3":
        vals = words.view(ml_dtypes.float8_e4m3fn).astype(np.float64)
    else:
        nib = np.empty((g, 128, n, 4), np.uint8)
        nib[..., 0::2] = words & 0xF
        nib[..., 1::2] = words >> 4
        vals = E2M1[nib]
    vals = vals * np.repeat(np.exp2(scales.astype(np.float64) - 127.0), 8, axis=1)[..., None]
    return vals.transpose(0, 1, 3, 2).reshape(g * 512, n)


D, T, I, Q, J, G, M = 512, 2048, 512, 128, 512, 64, 2048


def setup_inputs():
    n = np.random.standard_normal
    idx = np.random.permutation(T)[:I]
    idx2 = np.random.permutation(T)[:J]
    idx3 = np.random.permutation(M)[:I]
    fd = mx_kscale(D)
    fj = mx_kscale(J)
    keysp = pack_weight(n((D, T)) / fd[:, None], "e2m1")
    return {
        "query": (n((D, Q)) * 0.6 / np.sqrt(D) * fd[:, None]).astype(np.float32),
        "keys_words": keysp[0],
        "keys_scales": keysp[1],
        "hf": (np.random.uniform(0.5, 2.0, (J, 1)) * fj[:, None]).astype(np.float32),
        "mixer": (n((J, I)) * 0.05 / fj[:, None]).astype(np.float32),
        "cap": (np.random.uniform(0.01, 0.018, (Q, 1))).astype(np.float32),
        "old": (np.random.uniform(0.0, 2.0, (Q, M))).astype(np.float32),
        "fade": (np.random.uniform(0.3, 0.9, (Q, 1))).astype(np.float32),
        "offs": striped(idx),
        "offs2": striped(idx2),
        "offs3": striped(idx3),
    }


def reference(query, keys_words, keys_scales, hf, mixer, cap, old, fade, offs, offs2, offs3):
    idx = unstriped(offs)
    idx2 = unstriped(offs2)
    idx3 = unstriped(offs3)
    keysu = unpack_weight(keys_words, keys_scales, "e2m1")
    keysidx2g = keysu[:, idx2]
    queryq = mxq(f64(query), 0, "e4m3")
    a0 = keysidx2g.T @ queryq
    af = a0 * f64(hf)
    afq = mxq(af, 0, "e4m3")
    mixerq = mxq(f64(mixer), 0, "e4m3")
    mx0 = afq.T @ mixerq
    keysidxg = keysu[:, idx]
    a = queryq.T @ keysidxg
    s = a + mx0
    p = np.exp(s - np.max(s, axis=1, keepdims=True))
    r = p / np.sum(p, axis=1, keepdims=True)
    pg = r.reshape(Q, G, I // G).sum(axis=2)
    k0 = np.minimum(pg, f64(cap)) / pg
    kr = np.repeat(k0, I // G, axis=1)
    w = r * kr
    ws = w * 512.0
    wf = np.zeros((Q, M))
    wf[:, idx3] = ws
    y = f64(old) * f64(fade) + wf
    return y

@@ -1,0 +1,201 @@
+from contextlib import ExitStack
+
+import concourse.mybir as mybir
+from concourse.masks import make_identity
+
+D, T, I, Q, J, G, M = 512, 2048, 512, 128, 512, 64, 2048
+P = 128
+PACK = 4
+RUN = I // G
+HALF = I // 2
+FLOPS = 2 * D * J * Q + 2 * J * Q * I + 2 * D * Q * I
+
+F32 = mybir.dt.float32
+BF16 = mybir.dt.bfloat16
+I32 = mybir.dt.int32
+U32 = mybir.dt.uint32
+U16 = mybir.dt.uint16
+U8 = mybir.dt.uint8
+FP8X4 = mybir.dt.float8_e4m3fn_x4
+FP4X4 = mybir.dt.float4_e2m1fn_x4
+ALU = mybir.AluOpType
+ACT = mybir.ActivationFunctionType
+AX = mybir.AxisListType
+
+OUT_CHUNKS = (256, 512, 512, 512, 256)
+
+
+def tile_attend_mixedslots_runcap_counts_kernel(
+    tc, query, keys_words, keys_scales, hf, mixer, cap, old, fade, offs, offs2, offs3, out
+):
+    nc = tc.nc
+    with ExitStack() as ctx:
+        lists = ctx.enter_context(tc.tile_pool(name="lists", bufs=1))
+        sb = ctx.enter_context(tc.tile_pool(name="sb", bufs=1))
+        shared = ctx.enter_context(tc.tile_pool(name="shared", bufs=1))
+        ps = ctx.enter_context(tc.psum_pool(name="ps", bufs=1))
+
+        def tile(name, shape, dtype):
+            return sb.tile(shape, dtype, name=name, align_bytes=64)
+
+        def placed(name, shape, dtype, offset):
+            return shared.tile(shape, dtype, name=name, align_bytes=64, offset=offset)
+
+        offs_t = lists.tile([P, I // 16], U16, name="offs_t")
+        offs2_t = lists.tile([P, J // 16], U16, name="offs2_t")
+        offs3_t = lists.tile([P, I // 16], U16, name="offs3_t")
+
+        pool_words = tile("pool_words", [P, T], U16)
+        pool_scales = tile("pool_scales", [P, T], U8)
+        scattered = tile("scattered", [P, M], F32)
+        ident = tile("ident", [P, P], F32)
+        q_raw = placed("q_raw", [P, PACK, Q], F32, 0)
+        mix_raw = [placed("mix_raw%d" % h, [P, PACK, HALF], F32, 2048 + 4096 * h) for h in range(2)]
+        hf_t = tile("hf_t", [P, PACK], F32)
+        cap_t = tile("cap_t", [P, 1], F32)
+        fade_t = tile("fade_t", [P, 1], F32)
+        old_t = tile("old_t", [P, M], F32)
+
+        nc.gpsimd.memset(pool_scales[:].bitcast(I32), 0)
+        nc.vector.memset(scattered[:], 0.0)
+        make_identity(nc, ident[:])
+
+        mixer_rows = mixer.rearrange("(p t) i -> p t i", t=PACK)
+        nc.sync.dma_start(offs2_t[:], offs2)
+        nc.sync.dma_start(pool_words[:].bitcast(I32), keys_words[0].bitcast(I32))
+        for r in range(4):
+            nc.sync.dma_start(pool_scales[r:P:32, :].bitcast(I32), keys_scales[0, r:16:4, :].bitcast(I32))
+        nc.sync.dma_start(q_raw[:], query.rearrange("(p t) q -> p t q", t=PACK))
+        nc.sync.dma_start(mix_raw[0][:], mixer_rows[:, :, 0:HALF])
+        nc.sync.dma_start(offs_t[:], offs)
+        nc.sync.dma_start(mix_raw[1][:], mixer_rows[:, :, HALF:I])
+        nc.sync.dma_start(hf_t[:], hf.rearrange("(p t) o -> p (t o)", t=PACK))
+        nc.sync.dma_start(cap_t[:], cap)
+        nc.sync.dma_start(fade_t[:], fade)
+        nc.sync.dma_start(offs3_t[:], offs3)
+        nc.sync.dma_start(old_t[:], old)
+
+        def interleave(dst, src):
+            nc.scalar.copy(
+                dst.rearrange("p (c i) t -> p c t i", i=4), src.rearrange("p t (c i) -> p c t i", i=4)
+            )
+
+        def quantise(codes, scales, src):
+            nc.vector.quantize_mx(codes.bitcast(FP8X4), scales, src.rearrange("p c t -> p (c t)"))
+
+        q_bf = tile("q_bf", [P, Q, PACK], BF16)
+        q_codes = tile("q_codes", [P, Q], U32)
+        q_scales = tile("q_scales", [P, Q], U8)
+        mix_bf = [tile("mix_bf%d" % h, [P, HALF, PACK], BF16) for h in range(2)]
+        mix_codes = [tile("mix_codes0", [P, HALF], U32), placed("mix_codes1", [P, HALF], U32, 10240)]
+        mix_scales = [tile("mix_scales%d" % h, [P, HALF], U8) for h in range(2)]
+        mixed_words = tile("mixed_words", [P, J], U16)
+        mixed_scales = [tile("mixed_scales0", [P, HALF], U8), placed("mixed_scales1", [P, HALF], U8, 1024)]
+        own_words = placed("own_words", [P, I], U16, 0)
+        own_scales = [placed("own_scales0", [P, HALF], U8, 2048), placed("own_scales1", [P, HALF], U8, 11264)]
+
+        a0_ps = [ps.tile([P, HALF], F32, name="a0_ps%d" % h) for h in range(2)]
+        a0_turned = ps.tile([P, PACK, Q], F32, name="a0_turned")
+        s_ps = [ps.tile([P, HALF], F32, name="s_ps%d" % h) for h in range(2)]
+
+        interleave(q_bf[:], q_raw[:])
+        nc.vector.tensor_copy(mixed_words[:], pool_words[:].indirect(offs2_t[:]))
+
+        def scale_gather(dst, offsets, h):
+            cols = HALF // 16
+            nc.vector.tensor_copy(dst[h][:], pool_scales[:].indirect(offsets[:, h * cols : (h + 1) * cols]))
+
+        def first_pass(h):
+            nc.tensor.matmul_mx(
+                a0_ps[h][:], lhsT=q_codes[:].bitcast(FP8X4), lhsT_scale=q_scales[:],
+                rhs=mixed_words[:, h * HALF : (h + 1) * HALF].bitcast(FP4X4), rhs_scale=mixed_scales[h][:],
+                start=True, stop=True,
+            )
+
+        scale_gather(mixed_scales, offs2_t, 0)
+        quantise(q_codes[:], q_scales[:], q_bf[:])
+        first_pass(0)
+        scale_gather(mixed_scales, offs2_t, 1)
+        first_pass(1)
+        interleave(mix_bf[0][:], mix_raw[0][:])
+        nc.vector.tensor_copy(own_words[:], pool_words[:].indirect(offs_t[:]))
+
+        a0_dealt = placed("a0_dealt", [P, PACK, P], F32, 10240)
+        for h in range(2):
+            nc.scalar.copy(a0_dealt[:, :, h * 64 : (h + 1) * 64], a0_ps[h][:].rearrange("q (s t) -> q t s", t=PACK))
+        for t in range(PACK):
+            nc.tensor.transpose(a0_turned[:, t, :], a0_dealt[:, t, :], ident[:])
+        interleave(mix_bf[1][:], mix_raw[1][:])
+
+        def own_pass(h, start, stop):
+            nc.tensor.matmul_mx(
+                s_ps[h][:], lhsT=q_codes[:].bitcast(FP8X4), lhsT_scale=q_scales[:],
+                rhs=own_words[:, h * HALF : (h + 1) * HALF].bitcast(FP4X4), rhs_scale=own_scales[h][:],
+                start=start, stop=stop,
+            )
+
+        af_bf = tile("af_bf", [P, Q, PACK], BF16)
+        af_codes = tile("af_codes", [P, Q], U32)
+        af_scales = tile("af_scales", [P, Q], U8)
+
+        def mixed_pass(h, start, stop):
+            nc.tensor.matmul_mx(
+                s_ps[h][:], lhsT=af_codes[:].bitcast(FP8X4), lhsT_scale=af_scales[:],
+                rhs=mix_codes[h][:].bitcast(FP8X4), rhs_scale=mix_scales[h][:], start=start, stop=stop,
+            )
+
+        quantise(mix_codes[0][:], mix_scales[0][:], mix_bf[0][:])
+        scale_gather(own_scales, offs_t, 0)
+        own_pass(0, True, False)
+        nc.vector.tensor_tensor(
+            af_bf[:], a0_turned[:].rearrange("p t q -> p q t"),
+            hf_t[:].unsqueeze(1).to_broadcast([P, Q, PACK]), ALU.mult,
+        )
+        quantise(mix_codes[1][:], mix_scales[1][:], mix_bf[1][:])
+        quantise(af_codes[:], af_scales[:], af_bf[:])
+        mixed_pass(0, False, True)
+        mixed_pass(1, True, False)
+        scale_gather(own_scales, offs_t, 1)
+        own_pass(1, False, True)
+
+        neg_max0 = tile("neg_max0", [P, 1], F32)
+        neg_max = tile("neg_max", [P, 1], F32)
+        neg_s1 = tile("neg_s1", [P, HALF], F32)
+        nc.vector.tensor_reduce(neg_max0[:], s_ps[0][:], AX.X, ALU.max, negate=True)
+        nc.vector.tensor_scalar(
+            neg_s1[:], s_ps[1][:], -1.0, neg_max0[:], ALU.mult, ALU.min, accum_out=neg_max[:]
+        )
+
+        p_t = tile("p_t", [P, I], F32)
+        half_sums = tile("half_sums", [P, 2], F32)
+        sums = tile("sums", [P, G + 1], F32)
+        inv = tile("inv", [P, G + 1], F32)
+        nc.scalar.activation(p_t[:, 0:HALF], s_ps[0][:], ACT.Exp, bias=neg_max[:], scale=1.0, accum_out=half_sums[:, 0:1])
+        nc.scalar.activation(p_t[:, HALF:I], neg_s1[:], ACT.Exp, bias=neg_max[:], scale=-1.0, accum_out=half_sums[:, 1:2])
+        nc.scalar.activation(sums[:, G : G + 1], half_sums[:, 0:1], ACT.Identity, bias=half_sums[:, 1:2], scale=1.0)
+        p_512 = tile("p_512", [P, I], F32)
+        nc.scalar.activation(p_512[:], p_t[:], ACT.Copy, scale=512.0)
+
+        runs = p_t[:].rearrange("p (g r) -> p g r", r=RUN)
+        GH = G // 2
+        nc.vector.tensor_reduce(sums[:, 0:GH], runs[:, 0:GH, :], AX.X, ALU.add)
+        nc.vector.tensor_reduce(sums[:, GH:G], runs[:, GH:G, :], AX.X, ALU.add)
+        nc.vector.reciprocal(inv[:, 0:GH], sums[:, 0:GH])
+        nc.vector.reciprocal(inv[:, GH : G + 1], sums[:, GH : G + 1])
+        factor = tile("factor", [P, I], F32)
+        nc.vector.tensor_scalar(
+            factor[:].rearrange("p (g r) -> p g r", r=RUN),
+            inv[:, 0:G].unsqueeze(2).to_broadcast([P, G, RUN]),
+            cap_t[:], inv[:, G : G + 1], ALU.mult, ALU.min,
+        )
+        nc.vector.tensor_tensor(scattered[:].indirect(offs3_t[:]), p_512[:], factor[:], ALU.mult)
+
+        c0 = 0
+        for n, width in enumerate(OUT_CHUNKS):
+            cols = slice(c0, c0 + width)
+            result = tile("result%d" % n, [P, width], F32)
+            nc.vector.scalar_tensor_tensor(
+                result[:], old_t[:, cols], fade_t[:], scattered[:, cols], ALU.mult, ALU.add
+            )
+            nc.sync.dma_start(out[:, cols], result[:])
+            c0 = c0 + width

@@ -1,7 +1,6 @@
 from contextlib import ExitStack
 
 import concourse.mybir as mybir
-from concourse.masks import make_identity
 
 D, T, I, Q, J, G, M = 512, 2048, 512, 128, 512, 64, 2048
 P = 128
@@ -48,7 +47,6 @@ def tile_attend_mixedslots_runcap_counts_kernel(
         pool_words = tile("pool_words", [P, T], U16)
         pool_scales = tile("pool_scales", [P, T], U8)
         scattered = tile("scattered", [P, M], F32)
-        ident = tile("ident", [P, P], F32)
         q_raw = placed("q_raw", [P, PACK, Q], F32, 0)
         mix_raw = [placed("mix_raw%d" % h, [P, PACK, HALF], F32, 2048 + 4096 * h) for h in range(2)]
         hf_t = tile("hf_t", [P, PACK], F32)
@@ -56,9 +54,8 @@ def tile_attend_mixedslots_runcap_counts_kernel(
         fade_t = tile("fade_t", [P, 1], F32)
         old_t = tile("old_t", [P, M], F32)
 
-        nc.gpsimd.memset(pool_scales[:].bitcast(I32), 0)
+        nc.vector.memset(pool_scales[:].bitcast(I32), 0)
         nc.vector.memset(scattered[:], 0.0)
-        make_identity(nc, ident[:])
 
         mixer_rows = mixer.rearrange("(p t) i -> p t i", t=PACK)
         nc.sync.dma_start(offs2_t[:], offs2)
@@ -87,14 +84,14 @@ def tile_attend_mixedslots_runcap_counts_kernel(
         q_codes = tile("q_codes", [P, Q], U32)
         q_scales = tile("q_scales", [P, Q], U8)
         mix_bf = [tile("mix_bf%d" % h, [P, HALF, PACK], BF16) for h in range(2)]
-        mix_codes = [tile("mix_codes0", [P, HALF], U32), placed("mix_codes1", [P, HALF], U32, 10240)]
+        mix_codes = [tile("mix_codes%d" % h, [P, HALF], U32) for h in range(2)]
         mix_scales = [tile("mix_scales%d" % h, [P, HALF], U8) for h in range(2)]
         mixed_words = tile("mixed_words", [P, J], U16)
-        mixed_scales = [tile("mixed_scales0", [P, HALF], U8), placed("mixed_scales1", [P, HALF], U8, 1024)]
+        mixed_dealt = placed("mixed_dealt", [P, J], U16, 1024)
+        mixed_scales = tile("mixed_scales", [P, J], U8)
         own_words = placed("own_words", [P, I], U16, 0)
-        own_scales = [placed("own_scales0", [P, HALF], U8, 2048), placed("own_scales1", [P, HALF], U8, 11264)]
+        own_scales = [placed("own_scales0", [P, HALF], U8, 2048), placed("own_scales1", [P, HALF], U8, 6144)]
 
-        a0_ps = [ps.tile([P, HALF], F32, name="a0_ps%d" % h) for h in range(2)]
         a0_turned = ps.tile([P, PACK, Q], F32, name="a0_turned")
         s_ps = [ps.tile([P, HALF], F32, name="s_ps%d" % h) for h in range(2)]
 
@@ -105,26 +102,22 @@ def tile_attend_mixedslots_runcap_counts_kernel(
             cols = HALF // 16
             nc.vector.tensor_copy(dst[h][:], pool_scales[:].indirect(offsets[:, h * cols : (h + 1) * cols]))
 
-        def first_pass(h):
-            nc.tensor.matmul_mx(
-                a0_ps[h][:], lhsT=q_codes[:].bitcast(FP8X4), lhsT_scale=q_scales[:],
-                rhs=mixed_words[:, h * HALF : (h + 1) * HALF].bitcast(FP4X4), rhs_scale=mixed_scales[h][:],
-                start=True, stop=True,
-            )
-
-        scale_gather(mixed_scales, offs2_t, 0)
+        nc.vector.tensor_copy(
+            mixed_scales[:].rearrange("p (t s) -> p s t", t=PACK), pool_scales[:].indirect(offs2_t[:])
+        )
+        nc.vector.tensor_copy(
+            mixed_dealt[:].rearrange("p (t s) -> p t s", t=PACK), mixed_words[:].rearrange("p (s t) -> p t s", t=PACK)
+        )
         quantise(q_codes[:], q_scales[:], q_bf[:])
-        first_pass(0)
-        scale_gather(mixed_scales, offs2_t, 1)
-        first_pass(1)
+        for t in range(PACK):
+            cols = slice(t * P, (t + 1) * P)
+            nc.tensor.matmul_mx(
+                a0_turned[:, t, :], lhsT=mixed_dealt[:, cols].bitcast(FP4X4), lhsT_scale=mixed_scales[:, cols],
+                rhs=q_codes[:].bitcast(FP8X4), rhs_scale=q_scales[:], start=True, stop=True,
+            )
         interleave(mix_bf[0][:], mix_raw[0][:])
         nc.vector.tensor_copy(own_words[:], pool_words[:].indirect(offs_t[:]))
 
-        a0_dealt = placed("a0_dealt", [P, PACK, P], F32, 10240)
-        for h in range(2):
-            nc.scalar.copy(a0_dealt[:, :, h * 64 : (h + 1) * 64], a0_ps[h][:].rearrange("q (s t) -> q t s", t=PACK))
-        for t in range(PACK):
-            nc.tensor.transpose(a0_turned[:, t, :], a0_dealt[:, t, :], ident[:])
         interleave(mix_bf[1][:], mix_raw[1][:])
 
         def own_pass(h, start, stop):
@@ -144,50 +137,64 @@ def tile_attend_mixedslots_runcap_counts_kernel(
                 rhs=mix_codes[h][:].bitcast(FP8X4), rhs_scale=mix_scales[h][:], start=start, stop=stop,
             )
 
-        quantise(mix_codes[0][:], mix_scales[0][:], mix_bf[0][:])
-        scale_gather(own_scales, offs_t, 0)
-        own_pass(0, True, False)
         nc.vector.tensor_tensor(
             af_bf[:], a0_turned[:].rearrange("p t q -> p q t"),
             hf_t[:].unsqueeze(1).to_broadcast([P, Q, PACK]), ALU.mult,
         )
-        quantise(mix_codes[1][:], mix_scales[1][:], mix_bf[1][:])
+        quantise(mix_codes[0][:], mix_scales[0][:], mix_bf[0][:])
         quantise(af_codes[:], af_scales[:], af_bf[:])
+        scale_gather(own_scales, offs_t, 0)
+        own_pass(0, True, False)
         mixed_pass(0, False, True)
+        quantise(mix_codes[1][:], mix_scales[1][:], mix_bf[1][:])
         mixed_pass(1, True, False)
         scale_gather(own_scales, offs_t, 1)
         own_pass(1, False, True)
 
-        neg_max0 = tile("neg_max0", [P, 1], F32)
-        neg_max = tile("neg_max", [P, 1], F32)
-        neg_s1 = tile("neg_s1", [P, HALF], F32)
-        nc.vector.tensor_reduce(neg_max0[:], s_ps[0][:], AX.X, ALU.max, negate=True)
-        nc.vector.tensor_scalar(
-            neg_s1[:], s_ps[1][:], -1.0, neg_max0[:], ALU.mult, ALU.min, accum_out=neg_max[:]
-        )
-
+        neg_max = tile("neg_max", [P, 2], F32)
         p_t = tile("p_t", [P, I], F32)
-        half_sums = tile("half_sums", [P, 2], F32)
-        sums = tile("sums", [P, G + 1], F32)
-        inv = tile("inv", [P, G + 1], F32)
-        nc.scalar.activation(p_t[:, 0:HALF], s_ps[0][:], ACT.Exp, bias=neg_max[:], scale=1.0, accum_out=half_sums[:, 0:1])
-        nc.scalar.activation(p_t[:, HALF:I], neg_s1[:], ACT.Exp, bias=neg_max[:], scale=-1.0, accum_out=half_sums[:, 1:2])
-        nc.scalar.activation(sums[:, G : G + 1], half_sums[:, 0:1], ACT.Identity, bias=half_sums[:, 1:2], scale=1.0)
         p_512 = tile("p_512", [P, I], F32)
-        nc.scalar.activation(p_512[:], p_t[:], ACT.Copy, scale=512.0)
-
-        runs = p_t[:].rearrange("p (g r) -> p g r", r=RUN)
+        half_sums = tile("half_sums", [P, 2], F32)
+        shifts = tile("shifts", [P, 2], F32)
         GH = G // 2
-        nc.vector.tensor_reduce(sums[:, 0:GH], runs[:, 0:GH, :], AX.X, ALU.add)
-        nc.vector.tensor_reduce(sums[:, GH:G], runs[:, GH:G, :], AX.X, ALU.add)
-        nc.vector.reciprocal(inv[:, 0:GH], sums[:, 0:GH])
-        nc.vector.reciprocal(inv[:, GH : G + 1], sums[:, GH : G + 1])
+        sums = tile("sums", [P, G + 2], F32)
+        inv = tile("inv", [P, G + 2], F32)
         factor = tile("factor", [P, I], F32)
-        nc.vector.tensor_scalar(
-            factor[:].rearrange("p (g r) -> p g r", r=RUN),
-            inv[:, 0:G].unsqueeze(2).to_broadcast([P, G, RUN]),
-            cap_t[:], inv[:, G : G + 1], ALU.mult, ALU.min,
-        )
+        runs = p_t[:].rearrange("p (g r) -> p g r", r=RUN)
+        factor_runs = factor[:].rearrange("p (g r) -> p g r", r=RUN)
+
+        def col(t, c):
+            return t[:, c : c + 1]
+
+        def half(t, h):
+            return t[:, h * HALF : (h + 1) * HALF]
+
+        for h in range(2):
+            nc.vector.tensor_reduce(col(neg_max, h), s_ps[h][:], AX.X, ALU.max, negate=True)
+            nc.scalar.activation(
+                half(p_t, h), s_ps[h][:], ACT.Exp, bias=col(neg_max, h), scale=1.0, accum_out=col(half_sums, h)
+            )
+            if h == 0:
+                nc.scalar.activation(half(p_512, 0), half(p_t, 0), ACT.Copy, scale=512.0)
+        for h in range(2):
+            nc.scalar.activation(col(shifts, h), col(neg_max, 1 - h), ACT.Exp, bias=col(neg_max, h), scale=-1.0)
+        for h in range(2):
+            nc.scalar.activation(
+                col(sums, G + h), col(half_sums, 1 - h), ACT.Identity, bias=col(half_sums, h), scale=col(shifts, h)
+            )
+        nc.scalar.activation(half(p_512, 1), half(p_t, 1), ACT.Copy, scale=512.0)
+
+        nc.vector.tensor_reduce(sums[:, 0:GH], runs[:, 0:GH, :], AX.X, ALU.add)
+        nc.vector.reciprocal(inv[:, 0:GH], sums[:, 0:GH])
+        nc.vector.tensor_reduce(sums[:, GH:G], runs[:, GH:G, :], AX.X, ALU.add)
+        nc.vector.reciprocal(inv[:, G : G + 2], sums[:, G : G + 2])
+        nc.vector.reciprocal(inv[:, GH:G], sums[:, GH:G])
+        for h in range(2):
+            nc.vector.tensor_scalar(
+                factor_runs[:, h * GH : (h + 1) * GH, :],
+                inv[:, h * GH : (h + 1) * GH].unsqueeze(2).to_broadcast([P, GH, RUN]),
+                cap_t[:], col(inv, G + h), ALU.mult, ALU.min,
+            )
         nc.vector.tensor_tensor(scattered[:].indirect(offs3_t[:]), p_512[:], factor[:], ALU.mult)
 
         c0 = 0

@@ -1,6 +1,7 @@
 from contextlib import ExitStack
 
 import concourse.mybir as mybir
+from concourse.masks import make_identity
 
 D, T, I, Q, J, G, M = 512, 2048, 512, 128, 512, 64, 2048
 P = 128
@@ -21,7 +22,10 @@ ALU = mybir.AluOpType
 ACT = mybir.ActivationFunctionType
 AX = mybir.AxisListType
 
-OUT_CHUNKS = (256, 512, 512, 512, 256)
+BANK = 512
+VEC_BANKS = 3
+VEC_CHUNKS = (256, 256, 512, 256, 256)
+POOL_CHUNKS = (256, 256)
 
 
 def tile_attend_mixedslots_runcap_counts_kernel(
@@ -33,6 +37,8 @@ def tile_attend_mixedslots_runcap_counts_kernel(
         sb = ctx.enter_context(tc.tile_pool(name="sb", bufs=1))
         shared = ctx.enter_context(tc.tile_pool(name="shared", bufs=1))
         ps = ctx.enter_context(tc.psum_pool(name="ps", bufs=1))
+
+        late = ctx.enter_context(tc.psum_pool(name="late", bufs=1))
 
         def tile(name, shape, dtype):
             return sb.tile(shape, dtype, name=name, align_bytes=64)
@@ -55,18 +61,21 @@ def tile_attend_mixedslots_runcap_counts_kernel(
         old_t = tile("old_t", [P, M], F32)
 
         nc.vector.memset(pool_scales[:].bitcast(I32), 0)
+        ident = tile("ident", [P, P], F32)
+        nc.vector.memset(ident[:], 0.0)
+        make_identity(nc, ident[:], nomemset=True)
         nc.vector.memset(scattered[:], 0.0)
 
         mixer_rows = mixer.rearrange("(p t) i -> p t i", t=PACK)
-        nc.sync.dma_start(offs2_t[:], offs2)
         nc.sync.dma_start(pool_words[:].bitcast(I32), keys_words[0].bitcast(I32))
+        nc.sync.dma_start(offs2_t[:], offs2)
         for r in range(4):
             nc.sync.dma_start(pool_scales[r:P:32, :].bitcast(I32), keys_scales[0, r:16:4, :].bitcast(I32))
         nc.sync.dma_start(q_raw[:], query.rearrange("(p t) q -> p t q", t=PACK))
         nc.sync.dma_start(mix_raw[0][:], mixer_rows[:, :, 0:HALF])
         nc.sync.dma_start(offs_t[:], offs)
-        nc.sync.dma_start(mix_raw[1][:], mixer_rows[:, :, HALF:I])
         nc.sync.dma_start(hf_t[:], hf.rearrange("(p t) o -> p (t o)", t=PACK))
+        nc.sync.dma_start(mix_raw[1][:], mixer_rows[:, :, HALF:I])
         nc.sync.dma_start(cap_t[:], cap)
         nc.sync.dma_start(fade_t[:], fade)
         nc.sync.dma_start(offs3_t[:], offs3)
@@ -93,7 +102,9 @@ def tile_attend_mixedslots_runcap_counts_kernel(
         own_scales = [placed("own_scales0", [P, HALF], U8, 2048), placed("own_scales1", [P, HALF], U8, 6144)]
 
         a0_turned = ps.tile([P, PACK, Q], F32, name="a0_turned")
-        s_ps = [ps.tile([P, HALF], F32, name="s_ps%d" % h) for h in range(2)]
+        s_ps0 = ps.tile([P, HALF], F32, name="s_ps0")
+        s_ps1 = late.tile([P, 2 * BANK], F32, name="s_ps1", offset=0)
+        s_ps = [s_ps0[:], s_ps1[:, 0:HALF]]
 
         interleave(q_bf[:], q_raw[:])
         nc.vector.tensor_copy(mixed_words[:], pool_words[:].indirect(offs2_t[:]))
@@ -122,7 +133,7 @@ def tile_attend_mixedslots_runcap_counts_kernel(
 
         def own_pass(h, start, stop):
             nc.tensor.matmul_mx(
-                s_ps[h][:], lhsT=q_codes[:].bitcast(FP8X4), lhsT_scale=q_scales[:],
+                s_ps[h], lhsT=q_codes[:].bitcast(FP8X4), lhsT_scale=q_scales[:],
                 rhs=own_words[:, h * HALF : (h + 1) * HALF].bitcast(FP4X4), rhs_scale=own_scales[h][:],
                 start=start, stop=stop,
             )
@@ -133,18 +144,18 @@ def tile_attend_mixedslots_runcap_counts_kernel(
 
         def mixed_pass(h, start, stop):
             nc.tensor.matmul_mx(
-                s_ps[h][:], lhsT=af_codes[:].bitcast(FP8X4), lhsT_scale=af_scales[:],
+                s_ps[h], lhsT=af_codes[:].bitcast(FP8X4), lhsT_scale=af_scales[:],
                 rhs=mix_codes[h][:].bitcast(FP8X4), rhs_scale=mix_scales[h][:], start=start, stop=stop,
             )
 
+        quantise(mix_codes[0][:], mix_scales[0][:], mix_bf[0][:])
         nc.vector.tensor_tensor(
             af_bf[:], a0_turned[:].rearrange("p t q -> p q t"),
             hf_t[:].unsqueeze(1).to_broadcast([P, Q, PACK]), ALU.mult,
         )
-        quantise(mix_codes[0][:], mix_scales[0][:], mix_bf[0][:])
-        quantise(af_codes[:], af_scales[:], af_bf[:])
         scale_gather(own_scales, offs_t, 0)
         own_pass(0, True, False)
+        quantise(af_codes[:], af_scales[:], af_bf[:])
         mixed_pass(0, False, True)
         quantise(mix_codes[1][:], mix_scales[1][:], mix_bf[1][:])
         mixed_pass(1, True, False)
@@ -170,9 +181,9 @@ def tile_attend_mixedslots_runcap_counts_kernel(
             return t[:, h * HALF : (h + 1) * HALF]
 
         for h in range(2):
-            nc.vector.tensor_reduce(col(neg_max, h), s_ps[h][:], AX.X, ALU.max, negate=True)
+            nc.vector.tensor_reduce(col(neg_max, h), s_ps[h], AX.X, ALU.max, negate=True)
             nc.scalar.activation(
-                half(p_t, h), s_ps[h][:], ACT.Exp, bias=col(neg_max, h), scale=1.0, accum_out=col(half_sums, h)
+                half(p_t, h), s_ps[h], ACT.Exp, bias=col(neg_max, h), scale=1.0, accum_out=col(half_sums, h)
             )
             if h == 0:
                 nc.scalar.activation(half(p_512, 0), half(p_t, 0), ACT.Copy, scale=512.0)
@@ -197,12 +208,40 @@ def tile_attend_mixedslots_runcap_counts_kernel(
             )
         nc.vector.tensor_tensor(scattered[:].indirect(offs3_t[:]), p_512[:], factor[:], ALU.mult)
 
+        turned = [late.tile([P, BANK], F32, name="turned%d" % b, offset=2048 * b) for b in range(2)]
+        old_ps = [ps.tile([P, BANK], F32, name="old_ps%d" % b) for b in range(VEC_BANKS)]
+        old_turned = [placed("old_turned%d" % b, [P, BANK], F32, 10240 + 2048 * b) for b in range(VEC_BANKS)]
+
+        def turn(dst, src):
+            for k in range(BANK // P):
+                nc.tensor.transpose(dst[:, k * P : (k + 1) * P], src[:, k * P : (k + 1) * P], ident[:])
+
+        def staging(b):
+            return turned[b % 2][:, 0:BANK]
+
+        for b in range(VEC_BANKS + 1):
+            if b < VEC_BANKS:
+                turn(staging(b), old_t[:, b * BANK : (b + 1) * BANK])
+                nc.scalar.copy(old_turned[b][:], staging(b))
+            if b > 0:
+                turn(old_ps[b - 1][:], old_turned[b - 1][:])
+        pool0 = VEC_BANKS * BANK
+        faded = placed("faded", [P, M - pool0], F32, 10240)
+        nc.scalar.activation(faded[:], old_t[:, pool0:M], ACT.Copy, scale=fade_t[:])
+
         c0 = 0
-        for n, width in enumerate(OUT_CHUNKS):
+        g0 = 0
+        for n, width in enumerate(VEC_CHUNKS):
             cols = slice(c0, c0 + width)
             result = tile("result%d" % n, [P, width], F32)
             nc.vector.scalar_tensor_tensor(
-                result[:], old_t[:, cols], fade_t[:], scattered[:, cols], ALU.mult, ALU.add
+                result[:], old_ps[c0 // BANK][:, c0 % BANK : c0 % BANK + width], fade_t[:], scattered[:, cols], ALU.mult, ALU.add
             )
             nc.sync.dma_start(out[:, cols], result[:])
             c0 = c0 + width
+            if n < len(POOL_CHUNKS):
+                gw = POOL_CHUNKS[n]
+                gres = tile("gresult%d" % n, [P, gw], F32)
+                nc.gpsimd.tensor_tensor(gres[:], faded[:, g0 : g0 + gw], scattered[:, pool0 + g0 : pool0 + g0 + gw], ALU.add)
+                nc.scalar.dma_start(out[:, pool0 + g0 : pool0 + g0 + gw], gres[:])
+                g0 = g0 + gw

from contextlib import ExitStack

import concourse.mybir as mybir
from concourse.masks import make_identity

D, T, I, Q, J, G, M = 512, 2048, 512, 128, 512, 64, 2048
P = 128
PACK = 4
RUN = I // G
HALF = I // 2
FLOPS = 2 * D * J * Q + 2 * J * Q * I + 2 * D * Q * I

F32 = mybir.dt.float32
BF16 = mybir.dt.bfloat16
I32 = mybir.dt.int32
U32 = mybir.dt.uint32
U16 = mybir.dt.uint16
U8 = mybir.dt.uint8
FP8X4 = mybir.dt.float8_e4m3fn_x4
FP4X4 = mybir.dt.float4_e2m1fn_x4
ALU = mybir.AluOpType
ACT = mybir.ActivationFunctionType
AX = mybir.AxisListType

BANK = 512
VEC_BANKS = 3
VEC_CHUNKS = (256, 256, 512, 256, 256)
POOL_CHUNKS = (256, 256)


def tile_attend_mixedslots_runcap_counts_kernel(
    tc, query, keys_words, keys_scales, hf, mixer, cap, old, fade, offs, offs2, offs3, out
):
    nc = tc.nc
    with ExitStack() as ctx:
        lists = ctx.enter_context(tc.tile_pool(name="lists", bufs=1))
        sb = ctx.enter_context(tc.tile_pool(name="sb", bufs=1))
        shared = ctx.enter_context(tc.tile_pool(name="shared", bufs=1))
        ps = ctx.enter_context(tc.psum_pool(name="ps", bufs=1))

        late = ctx.enter_context(tc.psum_pool(name="late", bufs=1))

        def tile(name, shape, dtype):
            return sb.tile(shape, dtype, name=name, align_bytes=64)

        def placed(name, shape, dtype, offset):
            return shared.tile(shape, dtype, name=name, align_bytes=64, offset=offset)

        offs_t = lists.tile([P, I // 16], U16, name="offs_t")
        offs2_t = lists.tile([P, J // 16], U16, name="offs2_t")
        offs3_t = lists.tile([P, I // 16], U16, name="offs3_t")

        pool_words = tile("pool_words", [P, T], U16)
        pool_scales = tile("pool_scales", [P, T], U8)
        scattered = tile("scattered", [P, M], F32)
        q_raw = placed("q_raw", [P, PACK, Q], F32, 0)
        mix_raw = [placed("mix_raw%d" % h, [P, PACK, HALF], F32, 2048 + 4096 * h) for h in range(2)]
        hf_t = tile("hf_t", [P, PACK], F32)
        cap_t = tile("cap_t", [P, 1], F32)
        fade_t = tile("fade_t", [P, 1], F32)
        old_t = tile("old_t", [P, M], F32)

        nc.vector.memset(pool_scales[:].bitcast(I32), 0)
        ident = tile("ident", [P, P], F32)
        nc.vector.memset(ident[:], 0.0)
        make_identity(nc, ident[:], nomemset=True)
        nc.vector.memset(scattered[:], 0.0)

        mixer_rows = mixer.rearrange("(p t) i -> p t i", t=PACK)
        nc.sync.dma_start(pool_words[:].bitcast(I32), keys_words[0].bitcast(I32))
        nc.sync.dma_start(offs2_t[:], offs2)
        for r in range(4):
            nc.sync.dma_start(pool_scales[r:P:32, :].bitcast(I32), keys_scales[0, r:16:4, :].bitcast(I32))
        nc.sync.dma_start(q_raw[:], query.rearrange("(p t) q -> p t q", t=PACK))
        nc.sync.dma_start(mix_raw[0][:], mixer_rows[:, :, 0:HALF])
        nc.sync.dma_start(offs_t[:], offs)
        nc.sync.dma_start(hf_t[:], hf.rearrange("(p t) o -> p (t o)", t=PACK))
        nc.sync.dma_start(mix_raw[1][:], mixer_rows[:, :, HALF:I])
        nc.sync.dma_start(cap_t[:], cap)
        nc.sync.dma_start(fade_t[:], fade)
        nc.sync.dma_start(offs3_t[:], offs3)
        nc.sync.dma_start(old_t[:], old)

        def interleave(dst, src):
            nc.scalar.copy(
                dst.rearrange("p (c i) t -> p c t i", i=4), src.rearrange("p t (c i) -> p c t i", i=4)
            )

        def quantise(codes, scales, src):
            nc.vector.quantize_mx(codes.bitcast(FP8X4), scales, src.rearrange("p c t -> p (c t)"))

        q_bf = tile("q_bf", [P, Q, PACK], BF16)
        q_codes = tile("q_codes", [P, Q], U32)
        q_scales = tile("q_scales", [P, Q], U8)
        mix_bf = [tile("mix_bf%d" % h, [P, HALF, PACK], BF16) for h in range(2)]
        mix_codes = [tile("mix_codes%d" % h, [P, HALF], U32) for h in range(2)]
        mix_scales = [tile("mix_scales%d" % h, [P, HALF], U8) for h in range(2)]
        mixed_words = tile("mixed_words", [P, J], U16)
        mixed_dealt = placed("mixed_dealt", [P, J], U16, 1024)
        mixed_scales = tile("mixed_scales", [P, J], U8)
        own_words = placed("own_words", [P, I], U16, 0)
        own_scales = [placed("own_scales0", [P, HALF], U8, 2048), placed("own_scales1", [P, HALF], U8, 6144)]

        a0_turned = ps.tile([P, PACK, Q], F32, name="a0_turned")
        s_ps0 = ps.tile([P, HALF], F32, name="s_ps0")
        s_ps1 = late.tile([P, 2 * BANK], F32, name="s_ps1", offset=0)
        s_ps = [s_ps0[:], s_ps1[:, 0:HALF]]

        interleave(q_bf[:], q_raw[:])
        nc.vector.tensor_copy(mixed_words[:], pool_words[:].indirect(offs2_t[:]))

        def scale_gather(dst, offsets, h):
            cols = HALF // 16
            nc.vector.tensor_copy(dst[h][:], pool_scales[:].indirect(offsets[:, h * cols : (h + 1) * cols]))

        nc.vector.tensor_copy(
            mixed_scales[:].rearrange("p (t s) -> p s t", t=PACK), pool_scales[:].indirect(offs2_t[:])
        )
        nc.vector.tensor_copy(
            mixed_dealt[:].rearrange("p (t s) -> p t s", t=PACK), mixed_words[:].rearrange("p (s t) -> p t s", t=PACK)
        )
        quantise(q_codes[:], q_scales[:], q_bf[:])
        for t in range(PACK):
            cols = slice(t * P, (t + 1) * P)
            nc.tensor.matmul_mx(
                a0_turned[:, t, :], lhsT=mixed_dealt[:, cols].bitcast(FP4X4), lhsT_scale=mixed_scales[:, cols],
                rhs=q_codes[:].bitcast(FP8X4), rhs_scale=q_scales[:], start=True, stop=True,
            )
        interleave(mix_bf[0][:], mix_raw[0][:])
        nc.vector.tensor_copy(own_words[:], pool_words[:].indirect(offs_t[:]))

        interleave(mix_bf[1][:], mix_raw[1][:])

        def own_pass(h, start, stop):
            nc.tensor.matmul_mx(
                s_ps[h], lhsT=q_codes[:].bitcast(FP8X4), lhsT_scale=q_scales[:],
                rhs=own_words[:, h * HALF : (h + 1) * HALF].bitcast(FP4X4), rhs_scale=own_scales[h][:],
                start=start, stop=stop,
            )

        af_bf = tile("af_bf", [P, Q, PACK], BF16)
        af_codes = tile("af_codes", [P, Q], U32)
        af_scales = tile("af_scales", [P, Q], U8)

        def mixed_pass(h, start, stop):
            nc.tensor.matmul_mx(
                s_ps[h], lhsT=af_codes[:].bitcast(FP8X4), lhsT_scale=af_scales[:],
                rhs=mix_codes[h][:].bitcast(FP8X4), rhs_scale=mix_scales[h][:], start=start, stop=stop,
            )

        quantise(mix_codes[0][:], mix_scales[0][:], mix_bf[0][:])
        nc.vector.tensor_tensor(
            af_bf[:], a0_turned[:].rearrange("p t q -> p q t"),
            hf_t[:].unsqueeze(1).to_broadcast([P, Q, PACK]), ALU.mult,
        )
        scale_gather(own_scales, offs_t, 0)
        own_pass(0, True, False)
        quantise(af_codes[:], af_scales[:], af_bf[:])
        mixed_pass(0, False, True)
        quantise(mix_codes[1][:], mix_scales[1][:], mix_bf[1][:])
        mixed_pass(1, True, False)
        scale_gather(own_scales, offs_t, 1)
        own_pass(1, False, True)

        neg_max = tile("neg_max", [P, 2], F32)
        p_t = tile("p_t", [P, I], F32)
        p_512 = tile("p_512", [P, I], F32)
        half_sums = tile("half_sums", [P, 2], F32)
        shifts = tile("shifts", [P, 2], F32)
        GH = G // 2
        sums = tile("sums", [P, G + 2], F32)
        inv = tile("inv", [P, G + 2], F32)
        factor = tile("factor", [P, I], F32)
        runs = p_t[:].rearrange("p (g r) -> p g r", r=RUN)
        factor_runs = factor[:].rearrange("p (g r) -> p g r", r=RUN)

        def col(t, c):
            return t[:, c : c + 1]

        def half(t, h):
            return t[:, h * HALF : (h + 1) * HALF]

        for h in range(2):
            nc.vector.tensor_reduce(col(neg_max, h), s_ps[h], AX.X, ALU.max, negate=True)
            nc.scalar.activation(
                half(p_t, h), s_ps[h], ACT.Exp, bias=col(neg_max, h), scale=1.0, accum_out=col(half_sums, h)
            )
            if h == 0:
                nc.scalar.activation(half(p_512, 0), half(p_t, 0), ACT.Copy, scale=512.0)
        for h in range(2):
            nc.scalar.activation(col(shifts, h), col(neg_max, 1 - h), ACT.Exp, bias=col(neg_max, h), scale=-1.0)
        for h in range(2):
            nc.scalar.activation(
                col(sums, G + h), col(half_sums, 1 - h), ACT.Identity, bias=col(half_sums, h), scale=col(shifts, h)
            )
        nc.scalar.activation(half(p_512, 1), half(p_t, 1), ACT.Copy, scale=512.0)

        nc.vector.tensor_reduce(sums[:, 0:GH], runs[:, 0:GH, :], AX.X, ALU.add)
        nc.vector.reciprocal(inv[:, 0:GH], sums[:, 0:GH])
        nc.vector.tensor_reduce(sums[:, GH:G], runs[:, GH:G, :], AX.X, ALU.add)
        nc.vector.reciprocal(inv[:, G : G + 2], sums[:, G : G + 2])
        nc.vector.reciprocal(inv[:, GH:G], sums[:, GH:G])
        for h in range(2):
            nc.vector.tensor_scalar(
                factor_runs[:, h * GH : (h + 1) * GH, :],
                inv[:, h * GH : (h + 1) * GH].unsqueeze(2).to_broadcast([P, GH, RUN]),
                cap_t[:], col(inv, G + h), ALU.mult, ALU.min,
            )
        nc.vector.tensor_tensor(scattered[:].indirect(offs3_t[:]), p_512[:], factor[:], ALU.mult)

        turned = [late.tile([P, BANK], F32, name="turned%d" % b, offset=2048 * b) for b in range(2)]
        old_ps = [ps.tile([P, BANK], F32, name="old_ps%d" % b) for b in range(VEC_BANKS)]
        old_turned = [placed("old_turned%d" % b, [P, BANK], F32, 10240 + 2048 * b) for b in range(VEC_BANKS)]

        def turn(dst, src):
            for k in range(BANK // P):
                nc.tensor.transpose(dst[:, k * P : (k + 1) * P], src[:, k * P : (k + 1) * P], ident[:])

        def staging(b):
            return turned[b % 2][:, 0:BANK]

        for b in range(VEC_BANKS + 1):
            if b < VEC_BANKS:
                turn(staging(b), old_t[:, b * BANK : (b + 1) * BANK])
                nc.scalar.copy(old_turned[b][:], staging(b))
            if b > 0:
                turn(old_ps[b - 1][:], old_turned[b - 1][:])
        pool0 = VEC_BANKS * BANK
        faded = placed("faded", [P, M - pool0], F32, 10240)
        nc.scalar.activation(faded[:], old_t[:, pool0:M], ACT.Copy, scale=fade_t[:])

        c0 = 0
        g0 = 0
        for n, width in enumerate(VEC_CHUNKS):
            cols = slice(c0, c0 + width)
            result = tile("result%d" % n, [P, width], F32)
            nc.vector.scalar_tensor_tensor(
                result[:], old_ps[c0 // BANK][:, c0 % BANK : c0 % BANK + width], fade_t[:], scattered[:, cols], ALU.mult, ALU.add
            )
            nc.sync.dma_start(out[:, cols], result[:])
            c0 = c0 + width
            if n < len(POOL_CHUNKS):
                gw = POOL_CHUNKS[n]
                gres = tile("gresult%d" % n, [P, gw], F32)
                nc.gpsimd.tensor_tensor(gres[:], faded[:, g0 : g0 + gw], scattered[:, pool0 + g0 : pool0 + g0 + gw], ALU.add)
                nc.scalar.dma_start(out[:, pool0 + g0 : pool0 + g0 + gw], gres[:])
                g0 = g0 + gw
